import numpy as np
import ml_dtypes


def mxq(x, axis, fmt="e4m3"):
    dtype, down = {"e4m3": (ml_dtypes.float8_e4m3fn, 7), "e5m2": (ml_dtypes.float8_e5m2, 14)}[fmt]
    v = np.moveaxis(np.asarray(x, np.float32).astype(ml_dtypes.bfloat16).astype(np.float64), axis, -1)
    blocks = v.reshape(v.shape[:-1] + (-1, 32))
    amax = np.abs(blocks).max(-1, keepdims=True)
    byte = np.maximum(np.where(amax > 0, np.frexp(amax)[1] - 1 + 127, 0) - down, 1)
    scale = np.exp2(byte - 127.0)
    codes = (blocks / scale).astype(np.float32).astype(dtype).astype(np.float64)
    return np.moveaxis((codes * scale).reshape(v.shape), -1, axis)


WIDE = False


def mx_kscale(k):
    if not WIDE:
        return np.ones(k)
    levels = np.array([10, -10, 5, -5, 0])
    if k % 512:
        return np.exp2(np.random.permutation(np.resize(levels, k // 32))).repeat(32)
    a = np.empty((k // 512, 16))
    for p in range(k // 512):
        a[p, :8] = np.random.permutation(np.resize(levels, 8))
        for g in range(8):
            far = levels[np.abs(levels - a[p, g]) >= 10]
            a[p, g + 8] = far[np.random.randint(len(far))]
    return np.exp2(a.ravel()).repeat(32)


def f64(x):
    return np.asarray(x).astype(np.float64)


def striped(idx):
    return np.tile(idx.reshape(-1, 16).T, (8, 1)).astype(np.uint16)


def unstriped(offs):
    return offs[:16].T.reshape(-1).astype(np.int64)


def striped8(idx):
    return np.concatenate([x.reshape(-1, 16).T for x in idx]).astype(np.uint16)


def runs(offs, k):
    lists = np.stack([offs[16 * r : 16 * r + 16].T.reshape(-1) for r in range(8)]).astype(np.int64)
    return lists[np.arange(k) % 512 // 64]


def pack_weight(w):
    k, n = w.shape
    w = f64(np.asarray(w, np.float32).astype(ml_dtypes.bfloat16)).reshape(k // 32, 32, n)
    amax = np.abs(w).max(1)
    byte = np.clip(np.where(amax > 0, np.frexp(amax)[1] - 1 + 127 - 7, 1), 1, 254)
    scaled = (w * np.exp2(127.0 - byte)[:, None, :]).reshape(k, n).astype(np.float32)
    words = np.ascontiguousarray(scaled.reshape(k // 512, 128, 4, n).transpose(0, 1, 3, 2)).astype(ml_dtypes.float8_e4m3fn).view(np.uint8)
    return words, np.ascontiguousarray(byte.astype(np.uint8).reshape(k // 512, 16, n))


def unpack_weight(words, scales):
    g, p, n, _ = words.shape
    vals = np.ascontiguousarray(words).view(ml_dtypes.float8_e4m3fn).astype(np.float64) * np.repeat(np.exp2(scales.astype(np.float64) - 127.0), 8, axis=1)[..., None]
    return vals.transpose(0, 1, 3, 2).reshape(g * 512, n)

def planes(y):
    n, m = y.shape
    v = y.astype(np.float32).astype(ml_dtypes.bfloat16).astype(np.float64).reshape(n // 32, 32, m)
    top = np.abs(v).max(1)
    byte = np.clip(np.where(top > 0, np.frexp(top)[1] - 1 + 127 - 7, 1), 1, 254)
    codes = (v * np.exp2(127.0 - byte)[:, None, :]).reshape(n, m).astype(np.float32).astype(ml_dtypes.float8_e4m3fn).view(np.uint8)
    words = codes.reshape(n // 512, 128, 4, m).transpose(0, 1, 3, 2)
    return np.ascontiguousarray(words), np.ascontiguousarray(byte.astype(np.uint8).reshape(n // 512, 16, m))


K, T, S, G, H = 512, 2048, 512, 2048, 512


def setup_inputs():
    n = np.random.standard_normal
    s = mx_kscale(K)[:, None]
    packed_xT = pack_weight(n((K, T)) * s)
    packed_dT = pack_weight(n((K, G)) / s)
    return {
        "x_words": packed_xT[0],
        "x_scales": packed_xT[1],
        "d_words": packed_dT[0],
        "d_scales": packed_dT[1],
        "gs": (np.random.uniform(0.5, 1.5, (K, 1)) * s).astype(np.float32),
        "offs": striped(np.random.permutation(T)[:S]),
        "k1": striped8(np.random.randint(0, G, (8, H))),
        "nb": striped8(np.stack([np.random.permutation(S) for _ in range(8)])),
    }


def reference(x_words, x_scales, d_words, d_scales, gs, offs, k1, nb):
    d_k1 = unpack_weight(d_words, d_scales)[np.arange(K)[:, None], runs(k1, K)]
    xq = unpack_weight(x_words, x_scales)[:, unstriped(offs)]
    h = np.tanh(0.0625 * (d_k1.T @ xq))
    z = f64(gs) * (h[np.arange(H)[:, None], runs(nb, H)])
    h2 = 0.0625 * ((d_k1.T @ mxq(z, 0, "e4m3")))
    out_0 = h2
    return (out_0,) + planes(out_0)

@@ -1,0 +1,185 @@
+from contextlib import ExitStack
+
+import concourse.mybir as mybir
+
+F32 = mybir.dt.float32
+BF16 = mybir.dt.bfloat16
+I32 = mybir.dt.int32
+U32 = mybir.dt.uint32
+U16 = mybir.dt.uint16
+U8 = mybir.dt.uint8
+FP8X4 = mybir.dt.float8_e4m3fn_x4
+ACT = mybir.ActivationFunctionType
+MULT = mybir.AluOpType.mult
+
+P = 128
+PACK = 4
+TABLE = 2048
+S = 512
+FLOPS = 2 * 2 * 512 * 512 * 512
+CH = 128
+NCH = S // CH
+
+
+def tile_picked_pqtwice_tanh_po_kernel(
+    tc, x_words, x_scales, d_words, d_scales, gs, offs, k1, nb, out_0, out_1, out_2
+):
+    nc = tc.nc
+    with ExitStack() as ctx:
+        sb = ctx.enter_context(tc.tile_pool(name="sb", bufs=1))
+        ps = ctx.enter_context(tc.psum_pool(name="ps", bufs=1))
+
+        k1_t = sb.tile([P, S // 16], U16, name="k1_t")
+        offs_t = sb.tile([P, S // 16], U16, name="offs_t")
+        nb_t = sb.tile([P, S // 16], U16, name="nb_t")
+        d_tab = sb.tile([P, TABLE], I32, name="d_tab", align_bytes=64)
+        x_tab = sb.tile([P, TABLE], I32, name="x_tab", align_bytes=64)
+        d_sc_tab = sb.tile([P, TABLE], U8, name="d_sc_tab", align_bytes=64)
+        x_sc_tab = sb.tile([P, TABLE], U8, name="x_sc_tab", align_bytes=64)
+        gain = sb.tile([P, PACK], F32, name="gain")
+        planes = sb.tile([P, 2 * S], U8, name="planes", align_bytes=64)
+
+        nc.vector.memset(d_sc_tab[:].bitcast(I32), 0)
+        nc.vector.memset(x_sc_tab[:].bitcast(I32), 0)
+        nc.gpsimd.memset(planes[:].bitcast(I32), 0)
+        nc.sync.dma_start(k1_t[:], k1)
+        nc.scalar.dma_start(gain[:], gs.rearrange("(p t) o -> p (t o)", t=PACK))
+        nc.sync.dma_start(offs_t[:], offs)
+        nc.scalar.dma_start(d_sc_tab[0:P:8, :].bitcast(I32), d_scales[0].bitcast(I32))
+        nc.scalar.dma_start(x_sc_tab[0:P:8, :].bitcast(I32), x_scales[0].bitcast(I32))
+        nc.sync.dma_start(d_tab[:], d_words[0].rearrange("p n t -> p (n t)").bitcast(I32))
+        nc.sync.dma_start(nb_t[:], nb)
+        nc.sync.dma_start(x_tab[:], x_words[0].rearrange("p n t -> p (n t)").bitcast(I32))
+
+        GW = 128
+        gain_b = sb.tile([P, PACK, GW], F32, name="gain_b")
+        nc.scalar.activation(gain_b[:], gain[:].unsqueeze(2).to_broadcast([P, PACK, GW]), ACT.Copy)
+
+        d_sc_g = sb.tile([P, S], U8, name="d_sc_g", align_bytes=64)
+        x_sc_g = sb.tile([P, S], U8, name="x_sc_g", align_bytes=64)
+        both = sb.tile([P, 2 * S], U8, name="both", align_bytes=64)
+        nc.vector.tensor_copy(d_sc_g[:], d_sc_tab[:].indirect(k1_t[:]))
+        nc.vector.tensor_copy(
+            both[:, 0:S].rearrange("p (t c i) -> p c t i", t=PACK, i=16),
+            d_sc_g[:].rearrange("p (c i t) -> p c t i", t=PACK, i=16),
+        )
+        nc.vector.tensor_copy(x_sc_g[:], x_sc_tab[:].indirect(offs_t[:]))
+        nc.vector.tensor_copy(both[:, S : 2 * S].bitcast(I32), x_sc_g[:].bitcast(I32))
+        for b in range(4):
+            nc.scalar.dma_start(planes[b:P:32, :].bitcast(I32), both[8 * b : P : 32, :].bitcast(I32))
+
+        d_g = sb.tile([P, S], I32, name="d_g", align_bytes=64)
+        d_w = sb.tile([P, S], I32, name="d_w", align_bytes=64)
+        nc.vector.tensor_copy(d_g[:].bitcast(U32), d_tab[:].bitcast(U32).indirect(k1_t[:]))
+        nc.vector.tensor_copy(
+            d_w[:].rearrange("p (t c i) -> p c t i", t=PACK, i=4),
+            d_g[:].rearrange("p (c i t) -> p c t i", t=PACK, i=4),
+        )
+        HALF = S // 2
+        x_g = [sb.tile([P, HALF], I32, name="x_g%d" % u, align_bytes=64) for u in range(2)]
+        for u in range(2):
+            nc.vector.tensor_copy(x_g[u][:].bitcast(U32), x_tab[:].bitcast(U32).indirect(offs_t[:, 16 * u : 16 * (u + 1)]))
+
+        def product(out, t, rhs, rhs_scale):
+            nc.tensor.matmul_mx(
+                out=out,
+                lhsT=d_w[:, P * t : P * (t + 1)].bitcast(FP8X4),
+                lhsT_scale=planes[:, P * t : P * (t + 1)],
+                rhs=rhs.bitcast(FP8X4),
+                rhs_scale=rhs_scale,
+                start=True,
+                stop=True,
+            )
+
+        first = [ps.tile([P, HALF], F32, name="first%d" % u) for u in range(2)]
+        acc = [None] + [ps.tile([P, S], F32, name="acc%d" % t) for t in range(1, PACK)]
+        h = [sb.tile([P, S], F32, name="h%d" % t) for t in range(PACK)]
+        for u in range(2):
+            cols = slice(HALF * u, HALF * (u + 1))
+            for t in range(PACK):
+                dst = first[u][:] if t == 0 else acc[t][:, cols]
+                product(dst, t, x_g[u][:], planes[:, S + HALF * u : S + HALF * (u + 1)])
+                if t == 0:
+                    nc.scalar.activation(h[0][:, cols], first[u][:], ACT.Tanh, scale=0.0625)
+        for t in range(1, PACK):
+            nc.scalar.activation(h[t][:], acc[t][:], ACT.Tanh, scale=0.0625)
+
+        zg = [sb.tile([P, PACK, CH], F32, name="zg%d" % c) for c in range(NCH)]
+        y_words = sb.tile([P, S], I32, name="y_words", align_bytes=64)
+        y_scales = sb.tile([P, S], U8, name="y_scales", align_bytes=64)
+        out_rows = out_0.rearrange("(p t) j -> p t j", t=PACK)
+        words_out = out_1[0].rearrange("p n t -> p (n t)").bitcast(I32)
+
+        def gather(t, c):
+            nc.vector.tensor_tensor(zg[c][:, t, :], h[t][:].indirect(nb_t[:, 8 * c : 8 * (c + 1)]), gain_b[:, t, :], MULT)
+
+        zb = [sb.tile([P, CH * PACK], BF16, name="zb%d" % c, align_bytes=64) for c in range(NCH)]
+        z_w = [sb.tile([P, CH], I32, name="z_w%d" % c, align_bytes=64) for c in range(NCH)]
+        z_s = [sb.tile([P, CH], U8, name="z_s%d" % c, align_bytes=64) for c in range(NCH)]
+        acc2 = {}
+        y32 = [sb.tile([P, PACK, CH], F32, name="y32_%d" % c) for c in range(NCH)]
+        yb = [sb.tile([P, CH * PACK], BF16, name="yb%d" % c, align_bytes=64) for c in range(NCH)]
+
+        def weave(c, on_scalar):
+            dst = zb[c][:].rearrange("p (c i t) -> p c t i", t=PACK, i=4)
+            src = zg[c][:].rearrange("p t (c i) -> p c t i", i=4)
+            if on_scalar:
+                nc.scalar.copy(dst, src)
+            else:
+                nc.vector.tensor_copy(dst, src)
+
+        def second(c):
+            nc.vector.quantize_mx(out=z_w[c][:].bitcast(FP8X4), scales=z_s[c][:], in_=zb[c][:])
+            acc2[c] = ps.tile([P, PACK, CH], F32, name="bank2", tag="bank2", bufs=3)
+            for t in range(PACK):
+                product(acc2[c][:, t, :], t, z_w[c][:], z_s[c][:])
+
+        def out32(c):
+            nc.scalar.activation(y32[c][:], acc2[c][:], ACT.Copy, scale=0.0625)
+            nc.sync.dma_start(out_rows[:, :, CH * c : CH * (c + 1)], y32[c][:])
+
+        def out16(c, how):
+            if how == "s":
+                nc.scalar.activation(yb[c][:].rearrange("p (j t) -> p j t", t=PACK), acc2[c][:].rearrange("p t j -> p j t"), ACT.Copy, scale=0.0625)
+            elif how == "vp":
+                nc.vector.tensor_scalar(yb[c][:].rearrange("p (j t) -> p j t", t=PACK), acc2[c][:].rearrange("p t j -> p j t"), 0.0625, None, MULT)
+            else:
+                nc.vector.tensor_copy(
+                    yb[c][:].rearrange("p (c i t) -> p c t i", t=PACK, i=4), y32[c][:].rearrange("p t (c i) -> p c t i", i=4)
+                )
+
+        def outq(c):
+            cols = slice(CH * c, CH * (c + 1))
+            nc.vector.quantize_mx(out=y_words[:, cols].bitcast(FP8X4), scales=y_scales[:, cols], in_=yb[c][:])
+            nc.sync.dma_start(words_out[:, cols], y_words[:, cols])
+
+        for t in range(PACK):
+            for c in range(2):
+                gather(t, c)
+        weave(0, True)
+        weave(1, True)
+        second(0)
+        for t in range(PACK):
+            gather(t, 2)
+        second(1)
+        out32(0)
+        weave(2, True)
+        for t in range(PACK):
+            gather(t, 3)
+        out16(0, "s")
+        second(2)
+        weave(3, False)
+        out32(1)
+        out16(1, "s")
+        outq(0)
+        second(3)
+        out32(2)
+        outq(1)
+        out16(2, "vs")
+        outq(2)
+        out16(3, "vp")
+        out32(3)
+        outq(3)
+        for q in range(4):
+            eng = nc.scalar if q % 2 else nc.sync
+            eng.dma_start(out_2[0, 4 * q : 4 * q + 4, :].bitcast(I32), y_scales[32 * q : 32 * q + 4, :].bitcast(I32))

@@ -40,15 +40,14 @@ def tile_picked_pqtwice_tanh_po_kernel(
         planes = sb.tile([P, 2 * S], U8, name="planes", align_bytes=64)
 
         nc.vector.memset(d_sc_tab[:].bitcast(I32), 0)
-        nc.vector.memset(x_sc_tab[:].bitcast(I32), 0)
-        nc.gpsimd.memset(planes[:].bitcast(I32), 0)
+        nc.gpsimd.memset(x_sc_tab[:].bitcast(I32), 0)
         nc.sync.dma_start(k1_t[:], k1)
-        nc.scalar.dma_start(gain[:], gs.rearrange("(p t) o -> p (t o)", t=PACK))
         nc.sync.dma_start(offs_t[:], offs)
-        nc.scalar.dma_start(d_sc_tab[0:P:8, :].bitcast(I32), d_scales[0].bitcast(I32))
-        nc.scalar.dma_start(x_sc_tab[0:P:8, :].bitcast(I32), x_scales[0].bitcast(I32))
-        nc.sync.dma_start(d_tab[:], d_words[0].rearrange("p n t -> p (n t)").bitcast(I32))
         nc.sync.dma_start(nb_t[:], nb)
+        nc.sync.dma_start(gain[:], gs.rearrange("(p t) o -> p (t o)", t=PACK))
+        nc.sync.dma_start(d_sc_tab[0:P:8, :].bitcast(I32), d_scales[0].bitcast(I32))
+        nc.sync.dma_start(x_sc_tab[0:P:8, :].bitcast(I32), x_scales[0].bitcast(I32))
+        nc.sync.dma_start(d_tab[:], d_words[0].rearrange("p n t -> p (n t)").bitcast(I32))
         nc.sync.dma_start(x_tab[:], x_words[0].rearrange("p n t -> p (n t)").bitcast(I32))
 
         GW = 128
@@ -57,16 +56,15 @@ def tile_picked_pqtwice_tanh_po_kernel(
 
         d_sc_g = sb.tile([P, S], U8, name="d_sc_g", align_bytes=64)
         x_sc_g = sb.tile([P, S], U8, name="x_sc_g", align_bytes=64)
-        both = sb.tile([P, 2 * S], U8, name="both", align_bytes=64)
         nc.vector.tensor_copy(d_sc_g[:], d_sc_tab[:].indirect(k1_t[:]))
+        nc.vector.tensor_copy(x_sc_g[:], x_sc_tab[:].indirect(offs_t[:]))
         nc.vector.tensor_copy(
-            both[:, 0:S].rearrange("p (t c i) -> p c t i", t=PACK, i=16),
+            planes[:, 0:S].rearrange("p (t c i) -> p c t i", t=PACK, i=16),
             d_sc_g[:].rearrange("p (c i t) -> p c t i", t=PACK, i=16),
         )
-        nc.vector.tensor_copy(x_sc_g[:], x_sc_tab[:].indirect(offs_t[:]))
-        nc.vector.tensor_copy(both[:, S : 2 * S].bitcast(I32), x_sc_g[:].bitcast(I32))
-        for b in range(4):
-            nc.scalar.dma_start(planes[b:P:32, :].bitcast(I32), both[8 * b : P : 32, :].bitcast(I32))
+        nc.vector.tensor_copy(planes[:, S : 2 * S].bitcast(I32), x_sc_g[:].bitcast(I32))
+        for b in range(1, 4):
+            nc.scalar.dma_start(planes[b:P:32, :].bitcast(I32), planes[8 * b : P : 32, :].bitcast(I32))
 
         d_g = sb.tile([P, S], I32, name="d_g", align_bytes=64)
         d_w = sb.tile([P, S], I32, name="d_w", align_bytes=64)
@@ -94,23 +92,24 @@ def tile_picked_pqtwice_tanh_po_kernel(
         first = [ps.tile([P, HALF], F32, name="first%d" % u) for u in range(2)]
         acc = [None] + [ps.tile([P, S], F32, name="acc%d" % t) for t in range(1, PACK)]
         h = [sb.tile([P, S], F32, name="h%d" % t) for t in range(PACK)]
-        for u in range(2):
+        for t, u in ((0, 0), (1, 0), (0, 1), (1, 1), (2, 0), (2, 1), (3, 0), (3, 1)):
             cols = slice(HALF * u, HALF * (u + 1))
-            for t in range(PACK):
-                dst = first[u][:] if t == 0 else acc[t][:, cols]
-                product(dst, t, x_g[u][:], planes[:, S + HALF * u : S + HALF * (u + 1)])
-                if t == 0:
-                    nc.scalar.activation(h[0][:, cols], first[u][:], ACT.Tanh, scale=0.0625)
-        for t in range(1, PACK):
-            nc.scalar.activation(h[t][:], acc[t][:], ACT.Tanh, scale=0.0625)
+            dst = first[u][:] if t == 0 else acc[t][:, cols]
+            product(dst, t, x_g[u][:], planes[:, S + HALF * u : S + HALF * (u + 1)])
+            if t == 0:
+                nc.scalar.activation(h[0][:, cols], first[u][:], ACT.Tanh, scale=0.0625)
+            elif u == 1:
+                nc.scalar.activation(h[t][:], acc[t][:], ACT.Tanh, scale=0.0625)
 
-        zg = [sb.tile([P, PACK, CH], F32, name="zg%d" % c) for c in range(NCH)]
+        zg = {}
         y_words = sb.tile([P, S], I32, name="y_words", align_bytes=64)
         y_scales = sb.tile([P, S], U8, name="y_scales", align_bytes=64)
         out_rows = out_0.rearrange("(p t) j -> p t j", t=PACK)
         words_out = out_1[0].rearrange("p n t -> p (n t)").bitcast(I32)
 
         def gather(t, c):
+            if c not in zg:
+                zg[c] = sb.tile([P, PACK, CH], F32, name="zg", tag="zg", bufs=2)
             nc.vector.tensor_tensor(zg[c][:, t, :], h[t][:].indirect(nb_t[:, 8 * c : 8 * (c + 1)]), gain_b[:, t, :], MULT)
 
         zb = [sb.tile([P, CH * PACK], BF16, name="zb%d" % c, align_bytes=64) for c in range(NCH)]
@@ -134,6 +133,19 @@ def tile_picked_pqtwice_tanh_po_kernel(
             for t in range(PACK):
                 product(acc2[c][:, t, :], t, z_w[c][:], z_s[c][:])
 
+        def second_last(c):
+            nc.vector.quantize_mx(out=z_w[c][:].bitcast(FP8X4), scales=z_s[c][:], in_=zb[c][:])
+            banks = [ps.tile([P, 2, CH], F32, name="bank2", tag="bank2", bufs=3) for u in range(2)]
+            for t in range(PACK):
+                product(banks[t // 2][:, t % 2, :], t, z_w[c][:], z_s[c][:])
+            for u in range(2):
+                nc.vector.tensor_scalar(
+                    yb[c][:].rearrange("p (j t) -> p j t", t=PACK)[:, :, 2 * u : 2 * u + 2],
+                    banks[u][:].rearrange("p e j -> p j e"), 0.0625, None, MULT,
+                )
+                nc.scalar.activation(y32[c][:, 2 * u : 2 * u + 2, :], banks[u][:], ACT.Copy, scale=0.0625)
+            nc.scalar.dma_start(out_rows[:, :, CH * c : CH * (c + 1)], y32[c][:])
+
         def out32(c):
             nc.scalar.activation(y32[c][:], acc2[c][:], ACT.Copy, scale=0.0625)
             nc.sync.dma_start(out_rows[:, :, CH * c : CH * (c + 1)], y32[c][:])
@@ -151,34 +163,36 @@ def tile_picked_pqtwice_tanh_po_kernel(
         def outq(c):
             cols = slice(CH * c, CH * (c + 1))
             nc.vector.quantize_mx(out=y_words[:, cols].bitcast(FP8X4), scales=y_scales[:, cols], in_=yb[c][:])
-            nc.sync.dma_start(words_out[:, cols], y_words[:, cols])
+            if c >= NCH - 2:
+                done = slice(0, CH * (c + 1)) if c == NCH - 2 else cols
+                nc.sync.dma_start(words_out[:, done], y_words[:, done])
 
         for t in range(PACK):
             for c in range(2):
                 gather(t, c)
         weave(0, True)
-        weave(1, True)
+        weave(1, False)
         second(0)
-        for t in range(PACK):
-            gather(t, 2)
+        gather(0, 2)
         second(1)
+        for t in range(1, PACK):
+            gather(t, 2)
         out32(0)
         weave(2, True)
-        for t in range(PACK):
-            gather(t, 3)
         out16(0, "s")
+        for t in range(PACK - 1):
+            gather(t, 3)
         second(2)
-        weave(3, False)
+        gather(PACK - 1, 3)
         out32(1)
         out16(1, "s")
+        weave(3, False)
         outq(0)
-        second(3)
         out32(2)
         outq(1)
         out16(2, "vs")
+        second_last(3)
         outq(2)
-        out16(3, "vp")
-        out32(3)
         outq(3)
         for q in range(4):
             eng = nc.scalar if q % 2 else nc.sync

@@ -50,7 +50,7 @@ def tile_picked_pqtwice_tanh_po_kernel(
         nc.sync.dma_start(d_tab[:], d_words[0].rearrange("p n t -> p (n t)").bitcast(I32))
         nc.sync.dma_start(x_tab[:], x_words[0].rearrange("p n t -> p (n t)").bitcast(I32))
 
-        GW = 128
+        GW = 256
         gain_b = sb.tile([P, PACK, GW], F32, name="gain_b")
         nc.scalar.activation(gain_b[:], gain[:].unsqueeze(2).to_broadcast([P, PACK, GW]), ACT.Copy)
 
@@ -64,7 +64,7 @@ def tile_picked_pqtwice_tanh_po_kernel(
         )
         nc.vector.tensor_copy(planes[:, S : 2 * S].bitcast(I32), x_sc_g[:].bitcast(I32))
         for b in range(1, 4):
-            nc.scalar.dma_start(planes[b:P:32, :].bitcast(I32), planes[8 * b : P : 32, :].bitcast(I32))
+            (nc.scalar if b % 2 else nc.sync).dma_start(planes[b:P:32, :].bitcast(I32), planes[8 * b : P : 32, :].bitcast(I32))
 
         d_g = sb.tile([P, S], I32, name="d_g", align_bytes=64)
         d_w = sb.tile([P, S], I32, name="d_w", align_bytes=64)
@@ -92,7 +92,7 @@ def tile_picked_pqtwice_tanh_po_kernel(
         first = [ps.tile([P, HALF], F32, name="first%d" % u) for u in range(2)]
         acc = [None] + [ps.tile([P, S], F32, name="acc%d" % t) for t in range(1, PACK)]
         h = [sb.tile([P, S], F32, name="h%d" % t) for t in range(PACK)]
-        for t, u in ((0, 0), (1, 0), (0, 1), (1, 1), (2, 0), (2, 1), (3, 0), (3, 1)):
+        for t, u in ((0, 0), (0, 1), (1, 0), (1, 1), (2, 0), (2, 1), (3, 0), (3, 1)):
             cols = slice(HALF * u, HALF * (u + 1))
             dst = first[u][:] if t == 0 else acc[t][:, cols]
             product(dst, t, x_g[u][:], planes[:, S + HALF * u : S + HALF * (u + 1)])
@@ -101,16 +101,17 @@ def tile_picked_pqtwice_tanh_po_kernel(
             elif u == 1:
                 nc.scalar.activation(h[t][:], acc[t][:], ACT.Tanh, scale=0.0625)
 
-        zg = {}
+        zg = sb.tile([P, PACK, 2 * CH], F32, name="zg")
         y_words = sb.tile([P, S], I32, name="y_words", align_bytes=64)
         y_scales = sb.tile([P, S], U8, name="y_scales", align_bytes=64)
         out_rows = out_0.rearrange("(p t) j -> p t j", t=PACK)
         words_out = out_1[0].rearrange("p n t -> p (n t)").bitcast(I32)
 
-        def gather(t, c):
-            if c not in zg:
-                zg[c] = sb.tile([P, PACK, CH], F32, name="zg", tag="zg", bufs=2)
-            nc.vector.tensor_tensor(zg[c][:, t, :], h[t][:].indirect(nb_t[:, 8 * c : 8 * (c + 1)]), gain_b[:, t, :], MULT)
+        def gather(t, c, n=1):
+            at = CH * (c % 2)
+            nc.vector.tensor_tensor(
+                zg[:, t, at : at + n * CH], h[t][:].indirect(nb_t[:, 8 * c : 8 * (c + n)]), gain_b[:, t, 0 : n * CH], MULT
+            )
 
         zb = [sb.tile([P, CH * PACK], BF16, name="zb%d" % c, align_bytes=64) for c in range(NCH)]
         z_w = [sb.tile([P, CH], I32, name="z_w%d" % c, align_bytes=64) for c in range(NCH)]
@@ -121,7 +122,7 @@ def tile_picked_pqtwice_tanh_po_kernel(
 
         def weave(c, on_scalar):
             dst = zb[c][:].rearrange("p (c i t) -> p c t i", t=PACK, i=4)
-            src = zg[c][:].rearrange("p t (c i) -> p c t i", i=4)
+            src = zg[:, :, CH * (c % 2) : CH * (c % 2 + 1)].rearrange("p t (c i) -> p c t i", i=4)
             if on_scalar:
                 nc.scalar.copy(dst, src)
             else:
@@ -135,15 +136,22 @@ def tile_picked_pqtwice_tanh_po_kernel(
 
         def second_last(c):
             nc.vector.quantize_mx(out=z_w[c][:].bitcast(FP8X4), scales=z_s[c][:], in_=zb[c][:])
-            banks = [ps.tile([P, 2, CH], F32, name="bank2", tag="bank2", bufs=3) for u in range(2)]
+            banks = [ps.tile([P, 2, CH], F32, name="last%d" % u, tag="first%d" % u) for u in range(2)]
             for t in range(PACK):
                 product(banks[t // 2][:, t % 2, :], t, z_w[c][:], z_s[c][:])
-            for u in range(2):
+            def round_pair(u):
                 nc.vector.tensor_scalar(
                     yb[c][:].rearrange("p (j t) -> p j t", t=PACK)[:, :, 2 * u : 2 * u + 2],
                     banks[u][:].rearrange("p e j -> p j e"), 0.0625, None, MULT,
                 )
+
+            def copy_pair(u):
                 nc.scalar.activation(y32[c][:, 2 * u : 2 * u + 2, :], banks[u][:], ACT.Copy, scale=0.0625)
+
+            round_pair(0)
+            copy_pair(1)
+            copy_pair(0)
+            round_pair(1)
             nc.scalar.dma_start(out_rows[:, :, CH * c : CH * (c + 1)], y32[c][:])
 
         def out32(c):
@@ -167,11 +175,12 @@ def tile_picked_pqtwice_tanh_po_kernel(
                 done = slice(0, CH * (c + 1)) if c == NCH - 2 else cols
                 nc.sync.dma_start(words_out[:, done], y_words[:, done])
 
-        for t in range(PACK):
-            for c in range(2):
-                gather(t, c)
-        weave(0, True)
-        weave(1, False)
+        for t in range(PACK - 1):
+            gather(t, 0, 2)
+        gather(PACK - 1, 0)
+        gather(PACK - 1, 1)
+        weave(0, False)
+        weave(1, True)
         second(0)
         gather(0, 2)
         second(1)
@@ -189,9 +198,9 @@ def tile_picked_pqtwice_tanh_po_kernel(
         weave(3, False)
         outq(0)
         out32(2)
+        second_last(3)
         outq(1)
         out16(2, "vs")
-        second_last(3)
         outq(2)
         outq(3)
         for q in range(4):

@@ -39,7 +39,8 @@ def tile_picked_pqtwice_tanh_po_kernel(
         gain = sb.tile([P, PACK], F32, name="gain")
         planes = sb.tile([P, 2 * S], U8, name="planes", align_bytes=64)
 
-        nc.vector.memset(d_sc_tab[:].bitcast(I32), 0)
+        nc.vector.memset(d_sc_tab[:].bitcast(I32)[:, 0:257], 0)
+        nc.vector.memset(d_sc_tab[:].bitcast(I32)[:, 257:512], 0)
         nc.gpsimd.memset(x_sc_tab[:].bitcast(I32), 0)
         nc.sync.dma_start(k1_t[:], k1)
         nc.sync.dma_start(offs_t[:], offs)

from contextlib import ExitStack

import concourse.mybir as mybir

F32 = mybir.dt.float32
BF16 = mybir.dt.bfloat16
I32 = mybir.dt.int32
U32 = mybir.dt.uint32
U16 = mybir.dt.uint16
U8 = mybir.dt.uint8
FP8X4 = mybir.dt.float8_e4m3fn_x4
ACT = mybir.ActivationFunctionType
MULT = mybir.AluOpType.mult

P = 128
PACK = 4
TABLE = 2048
S = 512
FLOPS = 2 * 2 * 512 * 512 * 512
CH = 128
NCH = S // CH


def tile_picked_pqtwice_tanh_po_kernel(
    tc, x_words, x_scales, d_words, d_scales, gs, offs, k1, nb, out_0, out_1, out_2
):
    nc = tc.nc
    with ExitStack() as ctx:
        sb = ctx.enter_context(tc.tile_pool(name="sb", bufs=1))
        ps = ctx.enter_context(tc.psum_pool(name="ps", bufs=1))

        k1_t = sb.tile([P, S // 16], U16, name="k1_t")
        offs_t = sb.tile([P, S // 16], U16, name="offs_t")
        nb_t = sb.tile([P, S // 16], U16, name="nb_t")
        d_tab = sb.tile([P, TABLE], I32, name="d_tab", align_bytes=64)
        x_tab = sb.tile([P, TABLE], I32, name="x_tab", align_bytes=64)
        d_sc_tab = sb.tile([P, TABLE], U8, name="d_sc_tab", align_bytes=64)
        x_sc_tab = sb.tile([P, TABLE], U8, name="x_sc_tab", align_bytes=64)
        gain = sb.tile([P, PACK], F32, name="gain")
        planes = sb.tile([P, 2 * S], U8, name="planes", align_bytes=64)

        nc.vector.memset(d_sc_tab[:].bitcast(I32)[:, 0:257], 0)
        nc.vector.memset(d_sc_tab[:].bitcast(I32)[:, 257:512], 0)
        nc.gpsimd.memset(x_sc_tab[:].bitcast(I32), 0)
        nc.sync.dma_start(k1_t[:], k1)
        nc.sync.dma_start(offs_t[:], offs)
        nc.sync.dma_start(nb_t[:], nb)
        nc.sync.dma_start(gain[:], gs.rearrange("(p t) o -> p (t o)", t=PACK))
        nc.sync.dma_start(d_sc_tab[0:P:8, :].bitcast(I32), d_scales[0].bitcast(I32))
        nc.sync.dma_start(x_sc_tab[0:P:8, :].bitcast(I32), x_scales[0].bitcast(I32))
        nc.sync.dma_start(d_tab[:], d_words[0].rearrange("p n t -> p (n t)").bitcast(I32))
        nc.sync.dma_start(x_tab[:], x_words[0].rearrange("p n t -> p (n t)").bitcast(I32))

        GW = 256
        gain_b = sb.tile([P, PACK, GW], F32, name="gain_b")
        nc.scalar.activation(gain_b[:], gain[:].unsqueeze(2).to_broadcast([P, PACK, GW]), ACT.Copy)

        d_sc_g = sb.tile([P, S], U8, name="d_sc_g", align_bytes=64)
        x_sc_g = sb.tile([P, S], U8, name="x_sc_g", align_bytes=64)
        nc.vector.tensor_copy(d_sc_g[:], d_sc_tab[:].indirect(k1_t[:]))
        nc.vector.tensor_copy(x_sc_g[:], x_sc_tab[:].indirect(offs_t[:]))
        nc.vector.tensor_copy(
            planes[:, 0:S].rearrange("p (t c i) -> p c t i", t=PACK, i=16),
            d_sc_g[:].rearrange("p (c i t) -> p c t i", t=PACK, i=16),
        )
        nc.vector.tensor_copy(planes[:, S : 2 * S].bitcast(I32), x_sc_g[:].bitcast(I32))
        for b in range(1, 4):
            (nc.scalar if b % 2 else nc.sync).dma_start(planes[b:P:32, :].bitcast(I32), planes[8 * b : P : 32, :].bitcast(I32))

        d_g = sb.tile([P, S], I32, name="d_g", align_bytes=64)
        d_w = sb.tile([P, S], I32, name="d_w", align_bytes=64)
        nc.vector.tensor_copy(d_g[:].bitcast(U32), d_tab[:].bitcast(U32).indirect(k1_t[:]))
        nc.vector.tensor_copy(
            d_w[:].rearrange("p (t c i) -> p c t i", t=PACK, i=4),
            d_g[:].rearrange("p (c i t) -> p c t i", t=PACK, i=4),
        )
        HALF = S // 2
        x_g = [sb.tile([P, HALF], I32, name="x_g%d" % u, align_bytes=64) for u in range(2)]
        for u in range(2):
            nc.vector.tensor_copy(x_g[u][:].bitcast(U32), x_tab[:].bitcast(U32).indirect(offs_t[:, 16 * u : 16 * (u + 1)]))

        def product(out, t, rhs, rhs_scale):
            nc.tensor.matmul_mx(
                out=out,
                lhsT=d_w[:, P * t : P * (t + 1)].bitcast(FP8X4),
                lhsT_scale=planes[:, P * t : P * (t + 1)],
                rhs=rhs.bitcast(FP8X4),
                rhs_scale=rhs_scale,
                start=True,
                stop=True,
            )

        first = [ps.tile([P, HALF], F32, name="first%d" % u) for u in range(2)]
        acc = [None] + [ps.tile([P, S], F32, name="acc%d" % t) for t in range(1, PACK)]
        h = [sb.tile([P, S], F32, name="h%d" % t) for t in range(PACK)]
        for t, u in ((0, 0), (0, 1), (1, 0), (1, 1), (2, 0), (2, 1), (3, 0), (3, 1)):
            cols = slice(HALF * u, HALF * (u + 1))
            dst = first[u][:] if t == 0 else acc[t][:, cols]
            product(dst, t, x_g[u][:], planes[:, S + HALF * u : S + HALF * (u + 1)])
            if t == 0:
                nc.scalar.activation(h[0][:, cols], first[u][:], ACT.Tanh, scale=0.0625)
            elif u == 1:
                nc.scalar.activation(h[t][:], acc[t][:], ACT.Tanh, scale=0.0625)

        zg = sb.tile([P, PACK, 2 * CH], F32, name="zg")
        y_words = sb.tile([P, S], I32, name="y_words", align_bytes=64)
        y_scales = sb.tile([P, S], U8, name="y_scales", align_bytes=64)
        out_rows = out_0.rearrange("(p t) j -> p t j", t=PACK)
        words_out = out_1[0].rearrange("p n t -> p (n t)").bitcast(I32)

        def gather(t, c, n=1):
            at = CH * (c % 2)
            nc.vector.tensor_tensor(
                zg[:, t, at : at + n * CH], h[t][:].indirect(nb_t[:, 8 * c : 8 * (c + n)]), gain_b[:, t, 0 : n * CH], MULT
            )

        zb = [sb.tile([P, CH * PACK], BF16, name="zb%d" % c, align_bytes=64) for c in range(NCH)]
        z_w = [sb.tile([P, CH], I32, name="z_w%d" % c, align_bytes=64) for c in range(NCH)]
        z_s = [sb.tile([P, CH], U8, name="z_s%d" % c, align_bytes=64) for c in range(NCH)]
        acc2 = {}
        y32 = [sb.tile([P, PACK, CH], F32, name="y32_%d" % c) for c in range(NCH)]
        yb = [sb.tile([P, CH * PACK], BF16, name="yb%d" % c, align_bytes=64) for c in range(NCH)]

        def weave(c, on_scalar):
            dst = zb[c][:].rearrange("p (c i t) -> p c t i", t=PACK, i=4)
            src = zg[:, :, CH * (c % 2) : CH * (c % 2 + 1)].rearrange("p t (c i) -> p c t i", i=4)
            if on_scalar:
                nc.scalar.copy(dst, src)
            else:
                nc.vector.tensor_copy(dst, src)

        def second(c):
            nc.vector.quantize_mx(out=z_w[c][:].bitcast(FP8X4), scales=z_s[c][:], in_=zb[c][:])
            acc2[c] = ps.tile([P, PACK, CH], F32, name="bank2", tag="bank2", bufs=3)
            for t in range(PACK):
                product(acc2[c][:, t, :], t, z_w[c][:], z_s[c][:])

        def second_last(c):
            nc.vector.quantize_mx(out=z_w[c][:].bitcast(FP8X4), scales=z_s[c][:], in_=zb[c][:])
            banks = [ps.tile([P, 2, CH], F32, name="last%d" % u, tag="first%d" % u) for u in range(2)]
            for t in range(PACK):
                product(banks[t // 2][:, t % 2, :], t, z_w[c][:], z_s[c][:])
            def round_pair(u):
                nc.vector.tensor_scalar(
                    yb[c][:].rearrange("p (j t) -> p j t", t=PACK)[:, :, 2 * u : 2 * u + 2],
                    banks[u][:].rearrange("p e j -> p j e"), 0.0625, None, MULT,
                )

            def copy_pair(u):
                nc.scalar.activation(y32[c][:, 2 * u : 2 * u + 2, :], banks[u][:], ACT.Copy, scale=0.0625)

            round_pair(0)
            copy_pair(1)
            copy_pair(0)
            round_pair(1)
            nc.scalar.dma_start(out_rows[:, :, CH * c : CH * (c + 1)], y32[c][:])

        def out32(c):
            nc.scalar.activation(y32[c][:], acc2[c][:], ACT.Copy, scale=0.0625)
            nc.sync.dma_start(out_rows[:, :, CH * c : CH * (c + 1)], y32[c][:])

        def out16(c, how):
            if how == "s":
                nc.scalar.activation(yb[c][:].rearrange("p (j t) -> p j t", t=PACK), acc2[c][:].rearrange("p t j -> p j t"), ACT.Copy, scale=0.0625)
            elif how == "vp":
                nc.vector.tensor_scalar(yb[c][:].rearrange("p (j t) -> p j t", t=PACK), acc2[c][:].rearrange("p t j -> p j t"), 0.0625, None, MULT)
            else:
                nc.vector.tensor_copy(
                    yb[c][:].rearrange("p (c i t) -> p c t i", t=PACK, i=4), y32[c][:].rearrange("p t (c i) -> p c t i", i=4)
                )

        def outq(c):
            cols = slice(CH * c, CH * (c + 1))
            nc.vector.quantize_mx(out=y_words[:, cols].bitcast(FP8X4), scales=y_scales[:, cols], in_=yb[c][:])
            if c >= NCH - 2:
                done = slice(0, CH * (c + 1)) if c == NCH - 2 else cols
                nc.sync.dma_start(words_out[:, done], y_words[:, done])

        for t in range(PACK - 1):
            gather(t, 0, 2)
        gather(PACK - 1, 0)
        gather(PACK - 1, 1)
        weave(0, False)
        weave(1, True)
        second(0)
        gather(0, 2)
        second(1)
        for t in range(1, PACK):
            gather(t, 2)
        out32(0)
        weave(2, True)
        out16(0, "s")
        for t in range(PACK - 1):
            gather(t, 3)
        second(2)
        gather(PACK - 1, 3)
        out32(1)
        out16(1, "s")
        weave(3, False)
        outq(0)
        out32(2)
        second_last(3)
        outq(1)
        out16(2, "vs")
        outq(2)
        outq(3)
        for q in range(4):
            eng = nc.scalar if q % 2 else nc.sync
            eng.dma_start(out_2[0, 4 * q : 4 * q + 4, :].bitcast(I32), y_scales[32 * q : 32 * q + 4, :].bitcast(I32))
